import numpy as np
import ml_dtypes


def mxq(x, axis, fmt="e4m3"):
    dtype, down = {"e4m3": (ml_dtypes.float8_e4m3fn, 7), "e5m2": (ml_dtypes.float8_e5m2, 14)}[fmt]
    v = np.moveaxis(np.asarray(x, np.float32).astype(ml_dtypes.bfloat16).astype(np.float64), axis, -1)
    blocks = v.reshape(v.shape[:-1] + (-1, 32))
    amax = np.abs(blocks).max(-1, keepdims=True)
    byte = np.maximum(np.where(amax > 0, np.frexp(amax)[1] - 1 + 127, 0) - down, 1)
    scale = np.exp2(byte - 127.0)
    codes = (blocks / scale).astype(np.float32).astype(dtype).astype(np.float64)
    return np.moveaxis((codes * scale).reshape(v.shape), -1, axis)


WIDE = False


def mx_kscale(k):
    if not WIDE:
        return np.ones(k)
    levels = np.array([10, -10, 5, -5, 0])
    if k % 512:
        return np.exp2(np.random.permutation(np.resize(levels, k // 32))).repeat(32)
    a = np.empty((k // 512, 16))
    for p in range(k // 512):
        a[p, :8] = np.random.permutation(np.resize(levels, 8))
        for g in range(8):
            far = levels[np.abs(levels - a[p, g]) >= 10]
            a[p, g + 8] = far[np.random.randint(len(far))]
    return np.exp2(a.ravel()).repeat(32)


def f64(x):
    return np.asarray(x).astype(np.float64)


def striped(idx):
    return np.tile(np.asarray(idx).reshape(-1, 16).T, (8, 1)).astype(np.uint16)


def unstriped(offs):
    return offs[:16].T.reshape(-1).astype(np.int64)


def striped8(idx):
    return np.asarray(idx).reshape(8, -1, 16).transpose(0, 2, 1).reshape(128, -1).astype(np.uint16)


def unstriped8(offs):
    return offs.reshape(8, 16, -1).transpose(0, 2, 1).reshape(8, -1).astype(np.int64)


def pick8(x, idx, run):
    r = np.arange(len(x))
    return x[r[:, None], idx[r % (8 * run) // run]]


E2M1 = np.array([0.0, 0.5, 1.0, 1.5, 2.0, 3.0, 4.0, 6.0, -0.0, -0.5, -1.0, -1.5, -2.0, -3.0, -4.0, -6.0])


def pack_weight(w, fmt):
    k, n = w.shape
    w = f64(np.asarray(w, np.float32).astype(ml_dtypes.bfloat16)).reshape(k // 32, 32, n)
    amax = np.abs(w).max(1)
    if fmt == "e4m3":
        byte = np.frexp(amax)[1] - 1 + 127 - 7
    else:
        mant, ex = np.frexp(amax / 6.0)
        byte = np.where(mant > 0.5, ex, ex - 1) + 127
    byte = np.clip(np.where(amax > 0, byte, 1), 1, 254)
    scaled = (w * np.exp2(127.0 - byte)[:, None, :]).reshape(k, n).astype(np.float32)
    by_word = np.ascontiguousarray(scaled.reshape(k // 512, 128, 4, n).transpose(0, 1, 3, 2))
    if fmt == "e4m3":
        words = by_word.astype(ml_dtypes.float8_e4m3fn).view(np.uint8)
    else:
        c = by_word.astype(ml_dtypes.float4_e2m1fn).view(np.uint8) & 0xF
        words = (c[..., 0::2] | (c[..., 1::2] << 4)).reshape(k // 512, 128, 2 * n)
    return np.ascontiguousarray(words), np.ascontiguousarray(byte.astype(np.uint8).reshape(k // 512, 16, n))


def unpack_weight(words, scales, fmt):
    g, _, n = scales.shape
    words = np.ascontiguousarray(words).reshape(g, 128, n, -1)
    if fmt == "e4m3":
        vals = words.view(ml_dtypes.float8_e4m3fn).astype(np.float64)
    else:
        nib = np.empty((g, 128, n, 4), np.uint8)
        nib[..., 0::2] = words & 0xF
        nib[..., 1::2] = words >> 4
        vals = E2M1[nib]
    vals = vals * np.repeat(np.exp2(scales.astype(np.float64) - 127.0), 8, axis=1)[..., None]
    return vals.transpose(0, 1, 3, 2).reshape(g * 512, n)


K, J, R, T, F, Z, M, O, C, N = 512, 256, 512, 512, 2048, 512, 1024, 128, 512, 256


def setup_inputs():
    n = np.random.standard_normal
    idx = np.random.permutation(T)[:J]
    idx2 = np.stack([np.random.permutation(F)[:R] for _ in range(8)])
    idx3 = np.stack([np.random.permutation(F)[:R] for _ in range(8)])
    idx4 = np.random.permutation(M)[:J]
    idx5 = np.stack([np.random.permutation(C)[:J] for _ in range(8)])
    idx6 = np.stack([np.random.permutation(C)[:J] for _ in range(8)])
    idx7 = np.stack([np.random.permutation(J)[:O] for _ in range(8)])
    fk = mx_kscale(K)
    fz = mx_kscale(Z)
    fr = mx_kscale(R)
    xtp = pack_weight(n((K, T)) * fk[:, None], "e4m3")
    xop = pack_weight(n((Z, M)) / fz[:, None], "e4m3")
    w2p = pack_weight(n((Z, R)) * 1 / np.sqrt(Z) * fz[:, None], "e2m1")
    wbp = pack_weight(n((R, N)) * 1 / np.sqrt(R) / fr[:, None], "e2m1")
    return {
        "xt_words": xtp[0],
        "xt_scales": xtp[1],
        "ua": (np.random.randint(-7, 8, (K, F)).astype(np.float64)).astype(np.float32),
        "ha": ((np.random.randint(8, 19, (K, 1)) / 1024.0) / fk[:, None]).astype(np.float32),
        "hb": ((np.random.randint(8, 19, (K, 1)) / 1024.0) / fk[:, None]).astype(np.float32),
        "xo_words": xop[0],
        "xo_scales": xop[1],
        "w2_words": w2p[0],
        "w2_scales": w2p[1],
        "sa": (np.random.uniform(0.5, 1.6, (R, 1))).astype(np.float32),
        "sb": (np.random.uniform(0.5, 1.6, (R, 1)) * fr[:, None]).astype(np.float32),
        "wb_words": wbp[0],
        "wb_scales": wbp[1],
        "offs": striped(idx),
        "offs2": striped8(idx2),
        "offs3": striped8(idx3),
        "offs4": striped(idx4),
        "offs5": striped8(idx5),
        "offs6": striped8(idx6),
        "offs7": striped8(idx7),
    }


def reference(xt_words, xt_scales, ua, ha, hb, xo_words, xo_scales, w2_words, w2_scales, sa, sb, wb_words, wb_scales, offs, offs2, offs3, offs4, offs5, offs6, offs7):
    idx = unstriped(offs)
    idx2 = unstriped8(offs2)
    idx3 = unstriped8(offs3)
    idx4 = unstriped(offs4)
    idx5 = unstriped8(offs5)
    idx6 = unstriped8(offs6)
    idx7 = unstriped8(offs7)
    xtu = unpack_weight(xt_words, xt_scales, "e4m3")
    xou = unpack_weight(xo_words, xo_scales, "e4m3")
    w2u = unpack_weight(w2_words, w2_scales, "e2m1")
    wbu = unpack_weight(wb_words, wb_scales, "e2m1")
    wc = pick8(f64(ua), idx2, 64) * f64(ha) - pick8(f64(ua), idx3, 64) * f64(hb)
    wcq = mxq(wc, 0, "e4m3")
    xtidxg = xtu[:, idx]
    a = wcq.T @ xtidxg
    xoidx4g = xou[:, idx4]
    b = w2u.T @ xoidx4g
    pw = np.zeros((R, C))
    pw[np.arange(R)[:, None], idx5[np.arange(R) % 512 // 64]] = a
    g1 = np.maximum(pick8(pw, idx6, 64) * f64(sa), b)
    hid = pick8(g1, idx7, 64) * f64(sb)
    hidq = mxq(hid, 0, "e4m3")
    y = wbu.T @ hidq
    return y

@@ -1,0 +1,208 @@
+from contextlib import ExitStack
+
+import concourse.mybir as mybir
+
+K, J, R, T, F, Z, M, O, C, N = 512, 256, 512, 512, 2048, 512, 1024, 128, 512, 256
+FLOPS = 2 * (K * R * J + Z * R * J + R * N * O)
+
+F32 = mybir.dt.float32
+BF16 = mybir.dt.bfloat16
+I32 = mybir.dt.int32
+U32 = mybir.dt.uint32
+U16 = mybir.dt.uint16
+U8 = mybir.dt.uint8
+FP8X4 = mybir.dt.float8_e4m3fn_x4
+FP4X4 = mybir.dt.float4_e2m1fn_x4
+COPY = mybir.ActivationFunctionType.Copy
+SUBTRACT = mybir.AluOpType.subtract
+LARGER = mybir.AluOpType.max
+
+P = 128
+PACK = 4
+QUADRANT = 32
+
+
+def tile_picked_tokens_codegap_two_answered_one_plain_kernel(
+    tc, xt_words, xt_scales, ua, ha, hb, xo_words, xo_scales, w2_words, w2_scales, sa, sb, wb_words, wb_scales,
+    offs, offs2, offs3, offs4, offs5, offs6, offs7, out,
+):
+    nc = tc.nc
+    with ExitStack() as ctx:
+        keep = ctx.enter_context(tc.tile_pool(name="keep", bufs=1))
+        psum = ctx.enter_context(tc.psum_pool(name="psum", bufs=1))
+
+        def load_list(source, name):
+            tile = keep.tile(list(source.shape), U16, name=name)
+            nc.sync.dma_start(tile[:], source)
+            return tile
+
+        def load_rowwise(source, name, queue):
+            tile = keep.tile([P, PACK], F32, name=name)
+            queue.dma_start(tile[:], source.rearrange("(p t) one -> p (t one)", t=PACK))
+            return tile
+
+        def stage_scales(source, name, queue):
+            staged = keep.tile([PACK, PACK, source.shape[2] // 4], I32, name=name)
+            queue.dma_start(staged[:], source[0].bitcast(I32).rearrange("(q i) w -> i q w", i=PACK))
+            return staged
+
+        def spread_scales(staged, name):
+            plane = keep.tile([P, 4 * staged.shape[2]], U8, name=name, align_bytes=64)
+            nc.vector.memset(plane[:].bitcast(I32), 0)
+            for q in range(PACK):
+                nc.vector.tensor_copy(plane[QUADRANT * q : QUADRANT * q + PACK, :].bitcast(I32), staged[:, q, :])
+            return plane
+
+        def load_table(t):
+            tile = keep.tile([P, F], F32, name="table%d" % t)
+            nc.sync.dma_start(tile[:], ua.rearrange("(p t) f -> t p f", t=PACK)[t])
+            return tile
+
+        def load_words(source, name):
+            tile = keep.tile([P, source.shape[2]], U32, name=name, align_bytes=64)
+            nc.sync.dma_start(tile[:].bitcast(I32), source[0].rearrange("p c t -> p (c t)").bitcast(I32))
+            return tile
+
+        def load_nibbles(source, name):
+            tile = keep.tile([P, source.shape[2]], U8, name=name, align_bytes=64)
+            nc.sync.dma_start(tile[:].bitcast(I32), source[0].bitcast(I32))
+            return tile
+
+        tables = [load_table(0)]
+        step_a = load_rowwise(ha, "step_a", nc.scalar)
+        list2 = load_list(offs2, "list2")
+        step_b = load_rowwise(hb, "step_b", nc.scalar)
+        list3 = load_list(offs3, "list3")
+        xt_staged = stage_scales(xt_scales, "xt_staged", nc.scalar)
+        tables.append(load_table(1))
+        xo_staged = stage_scales(xo_scales, "xo_staged", nc.scalar)
+        list1 = load_list(offs, "list1")
+        w2_staged = stage_scales(w2_scales, "w2_staged", nc.sync)
+        tables.append(load_table(2))
+        list4 = load_list(offs4, "list4")
+        list5 = load_list(offs5, "list5")
+        tables.append(load_table(3))
+        xt_all = load_words(xt_words, "xt_all")
+        xo_all = load_words(xo_words, "xo_all")
+        list6 = load_list(offs6, "list6")
+        list7 = load_list(offs7, "list7")
+        w2_plain = load_nibbles(w2_words, "w2_plain")
+        wb_codes = load_nibbles(wb_words, "wb_codes")
+
+        weight_a = load_rowwise(sa, "weight_a", nc.gpsimd)
+        weight_b = load_rowwise(sb, "weight_b", nc.gpsimd)
+        wb_plane = keep.tile([P, N], U8, align_bytes=64)
+        nc.vector.memset(wb_plane[:].bitcast(I32), 0)
+        for q in range(PACK):
+            nc.gpsimd.dma_start(
+                wb_plane[QUADRANT * q : QUADRANT * q + PACK, :].bitcast(I32),
+                wb_scales[0, PACK * q : PACK * (q + 1), :].bitcast(I32),
+            )
+        boards = []
+        for t in range(PACK):
+            board = keep.tile([P, C], F32, name="board%d" % t)
+            nc.vector.memset(board[:], 0.0)
+            boards.append(board)
+        xt_plane_all = spread_scales(xt_staged, "xt_plane_all")
+        xo_plane_all = spread_scales(xo_staged, "xo_plane_all")
+        w2_plane_plain = spread_scales(w2_staged, "w2_plane_plain")
+
+        xt_plane = keep.tile([P, J], U8, align_bytes=64)
+        nc.vector.tensor_copy(xt_plane[:], xt_plane_all[:].indirect(list1[:]))
+        w2_plane = keep.tile([P, R], U8, align_bytes=64)
+        nc.vector.tensor_copy(
+            w2_plane[:].rearrange("p (t m) -> p t m", t=PACK), w2_plane_plain[:].rearrange("p (m t) -> p t m", t=PACK)
+        )
+        xo_plane = keep.tile([P, J], U8, align_bytes=64)
+        nc.vector.tensor_copy(xo_plane[:], xo_plane_all[:].indirect(list4[:]))
+
+        grouped = [keep.tile([P, P, PACK], BF16, name="grouped%d" % u, align_bytes=64) for u in range(PACK)]
+        paired = [None] + [keep.tile([P, 2, P, 2], BF16, name="paired%d" % u) for u in range(1, PACK)]
+        wc_codes = [keep.tile([P, P], U32, name="wc_codes%d" % u, align_bytes=64) for u in range(PACK)]
+        wc_plane = [keep.tile([P, P], U8, name="wc_plane%d" % u, align_bytes=64) for u in range(PACK)]
+        xt_codes = keep.tile([P, J], U32, align_bytes=64)
+        xo_codes = keep.tile([P, J], U32, align_bytes=64)
+        first_sb = []
+
+        def take_off(t, u, plus, minus):
+            target = grouped[0][:, :, t] if u == 0 else paired[u][:, t // 2, :, t % 2]
+            nc.vector.tensor_tensor(target, plus[:, u::PACK], minus[:, u::PACK], SUBTRACT)
+
+        for t in range(PACK):
+            plus = keep.tile([P, R], F32, name="plus%d" % t, tag="plus%d" % t, align_bytes=64)
+            minus = keep.tile([P, R], F32, name="minus%d" % t)
+            nc.scalar.activation(plus[:], tables[t][:].indirect(list2[:]), COPY, scale=step_a[:, t : t + 1])
+            nc.scalar.activation(minus[:], tables[t][:].indirect(list3[:]), COPY, scale=step_b[:, t : t + 1])
+            if t == PACK - 1:
+                nc.vector.tensor_copy(xt_codes[:], xt_all[:].indirect(list1[:]))
+                nc.vector.tensor_copy(xo_codes[:], xo_all[:].indirect(list4[:]))
+            if t < PACK - 1:
+                for u in range(PACK):
+                    take_off(t, u, plus, minus)
+        for u in range(PACK):
+            take_off(PACK - 1, u, plus, minus)
+            if u > 0:
+                nc.scalar.copy(
+                    grouped[u][:].rearrange("p m t -> p (m t)").bitcast(U32).rearrange("p (m h) -> p m h", h=2),
+                    paired[u][:].rearrange("p h m e -> p (h m e)").bitcast(U32).rearrange("p (h m) -> p m h", h=2),
+                )
+            nc.vector.quantize_mx(
+                out=wc_codes[u][:].bitcast(FP8X4), scales=wc_plane[u][:], in_=grouped[u][:].rearrange("p m t -> p (m t)")
+            )
+            first = psum.tile([P, J], F32, name="first%d" % u)
+            nc.tensor.matmul_mx(
+                out=first[:], lhsT=wc_codes[u][:].bitcast(FP8X4), lhsT_scale=wc_plane[u][:],
+                rhs=xt_codes[:].bitcast(FP8X4), rhs_scale=xt_plane[:], start=True, stop=True,
+            )
+            staged = keep.tile([P, J], F32, name="first_sb%d" % u)
+            nc.scalar.copy(staged[:], first[:])
+            first_sb.append(staged)
+
+        w2_codes = keep.tile([P, 2 * R], U8, name="w2_codes", tag="plus%d" % (PACK - 1), align_bytes=64)
+        nc.scalar.copy(
+            w2_codes[:].bitcast(U16).rearrange("p (t m) -> p t m", t=PACK),
+            w2_plain[:].bitcast(U16).rearrange("p (m t) -> p t m", t=PACK),
+        )
+        second = [psum.tile([P, 2, J], F32, name="second%d" % h) for h in range(2)]
+        for u in range(PACK):
+            nc.tensor.matmul_mx(
+                out=second[u // 2][:, u % 2, :], lhsT=w2_codes[:, 2 * P * u : 2 * P * (u + 1)].bitcast(FP4X4),
+                lhsT_scale=w2_plane[:, P * u : P * (u + 1)],
+                rhs=xo_codes[:].bitcast(FP8X4), rhs_scale=xo_plane[:], start=True, stop=True,
+            )
+
+        for u in range(PACK):
+            nc.vector.tensor_copy(boards[u][:].indirect(list5[:]), first_sb[u][:])
+        read = []
+        for u in range(PACK):
+            tile = keep.tile([P, J], F32, name="read%d" % u)
+            nc.scalar.activation(tile[:], boards[u][:].indirect(list6[:]), COPY, scale=weight_a[:, u : u + 1])
+            read.append(tile)
+        hid = keep.tile([P, PACK, O], BF16)
+        for u in range(PACK):
+            answer = keep.tile([P, J], F32, name="answer%d" % u)
+            nc.vector.tensor_tensor(answer[:], read[u][:], second[u // 2][:, u % 2, :], LARGER)
+            nc.scalar.activation(hid[:, u, :], answer[:].indirect(list7[:]), COPY, scale=weight_b[:, u : u + 1])
+
+        hid_grouped = keep.tile([P, O, PACK], BF16, align_bytes=64)
+        nc.vector.tensor_copy(hid_grouped[:, :, : PACK - 1], hid[:, : PACK - 1, :].rearrange("p t o -> p o t"))
+        nc.vector.tensor_copy(hid_grouped[:, :, PACK - 1], hid[:, PACK - 1, :])
+        hid_codes = keep.tile([P, O], U32, align_bytes=64)
+        hid_plane = keep.tile([P, O], U8, align_bytes=64)
+        nc.vector.quantize_mx(
+            out=hid_codes[:].bitcast(FP8X4), scales=hid_plane[:], in_=hid_grouped[:].rearrange("p o t -> p (o t)")
+        )
+        for h in range(N // P):
+            result = psum.tile([P, O], F32, name="result%d" % h)
+            nc.tensor.matmul_mx(
+                out=result[:], lhsT=wb_codes[:, 2 * P * h : 2 * P * (h + 1)].bitcast(FP4X4),
+                lhsT_scale=wb_plane[:, P * h : P * (h + 1)],
+                rhs=hid_codes[:].bitcast(FP8X4), rhs_scale=hid_plane[:], start=True, stop=True,
+            )
+            result_sb = keep.tile([P, O], F32, name="result_sb%d" % h)
+            if h == 0:
+                nc.scalar.copy(result_sb[:], result[:])
+                nc.scalar.dma_start(out[P * h : P * (h + 1), :], result_sb[:])
+            else:
+                nc.vector.tensor_copy(result_sb[:], result[:])
+                nc.sync.dma_start(out[P * h : P * (h + 1), :], result_sb[:])

@@ -68,6 +68,9 @@ def tile_picked_tokens_codegap_two_answered_one_plain_kernel(
             nc.sync.dma_start(tile[:].bitcast(I32), source[0].bitcast(I32))
             return tile
 
+        warm = keep.tile([P, 2], F32)
+        nc.vector.memset(warm[:, 0:1], 0.0)
+        nc.scalar.activation(warm[:, 1:2], warm[:, 0:1], COPY)
         tables = [load_table(0)]
         step_a = load_rowwise(ha, "step_a", nc.scalar)
         list2 = load_list(offs2, "list2")

@@ -20,6 +20,7 @@ LARGER = mybir.AluOpType.max
 P = 128
 PACK = 4
 QUADRANT = 32
+APART = 8
 
 
 def tile_picked_tokens_codegap_two_answered_one_plain_kernel(
@@ -41,16 +42,25 @@ def tile_picked_tokens_codegap_two_answered_one_plain_kernel(
             queue.dma_start(tile[:], source.rearrange("(p t) one -> p (t one)", t=PACK))
             return tile
 
-        def stage_scales(source, name, queue):
-            staged = keep.tile([PACK, PACK, source.shape[2] // 4], I32, name=name)
-            queue.dma_start(staged[:], source[0].bitcast(I32).rearrange("(q i) w -> i q w", i=PACK))
-            return staged
+        def load_scales_apart(source, name, queue):
+            tile = keep.tile([P, source.shape[2]], U8, name=name, align_bytes=64)
+            nc.gpsimd.memset(tile[:].bitcast(I32), 0)
+            queue.dma_start(tile[::APART, :].bitcast(I32), source[0].bitcast(I32))
+            return tile
 
-        def spread_scales(staged, name):
-            plane = keep.tile([P, 4 * staged.shape[2]], U8, name=name, align_bytes=64)
+        def load_plane(source, name):
+            plane = keep.tile([P, source.shape[2]], U8, name=name, align_bytes=64)
+            nc.gpsimd.memset(plane[:].bitcast(I32), 0)
+            rows = source[0].bitcast(I32).rearrange("(q i) w -> i q w", i=PACK)
+            for i in range(PACK):
+                nc.sync.dma_start(plane[i::QUADRANT, :].bitcast(I32), rows[i])
+            return plane
+
+        def close_up(apart, name):
+            plane = keep.tile(list(apart.shape), U8, name=name, align_bytes=64)
             nc.vector.memset(plane[:].bitcast(I32), 0)
-            for q in range(PACK):
-                nc.vector.tensor_copy(plane[QUADRANT * q : QUADRANT * q + PACK, :].bitcast(I32), staged[:, q, :])
+            for q in range(0, P, QUADRANT):
+                nc.gpsimd.dma_start(plane[q : q + PACK, :].bitcast(I32), apart[q : q + QUADRANT : APART, :].bitcast(I32))
             return plane
 
         def load_table(t):
@@ -76,48 +86,41 @@ def tile_picked_tokens_codegap_two_answered_one_plain_kernel(
         list2 = load_list(offs2, "list2")
         step_b = load_rowwise(hb, "step_b", nc.scalar)
         list3 = load_list(offs3, "list3")
-        xt_staged = stage_scales(xt_scales, "xt_staged", nc.scalar)
-        tables.append(load_table(1))
-        xo_staged = stage_scales(xo_scales, "xo_staged", nc.scalar)
         list1 = load_list(offs, "list1")
-        w2_staged = stage_scales(w2_scales, "w2_staged", nc.sync)
-        tables.append(load_table(2))
+        xt_scales_all = load_scales_apart(xt_scales, "xt_scales_all", nc.scalar)
+        tables.append(load_table(1))
         list4 = load_list(offs4, "list4")
-        list5 = load_list(offs5, "list5")
+        xo_scales_all = load_scales_apart(xo_scales, "xo_scales_all", nc.sync)
+        w2_plane_plain = load_plane(w2_scales, "w2_plane_plain")
+        tables.append(load_table(2))
         tables.append(load_table(3))
         xt_all = load_words(xt_words, "xt_all")
         xo_all = load_words(xo_words, "xo_all")
+        list5 = load_list(offs5, "list5")
+        w2_plain = load_nibbles(w2_words, "w2_plain")
+        weight_a = load_rowwise(sa, "weight_a", nc.sync)
         list6 = load_list(offs6, "list6")
         list7 = load_list(offs7, "list7")
-        w2_plain = load_nibbles(w2_words, "w2_plain")
+        weight_b = load_rowwise(sb, "weight_b", nc.sync)
         wb_codes = load_nibbles(wb_words, "wb_codes")
+        wb_plane = load_plane(wb_scales, "wb_plane")
 
-        weight_a = load_rowwise(sa, "weight_a", nc.gpsimd)
-        weight_b = load_rowwise(sb, "weight_b", nc.gpsimd)
-        wb_plane = keep.tile([P, N], U8, align_bytes=64)
-        nc.vector.memset(wb_plane[:].bitcast(I32), 0)
-        for q in range(PACK):
-            nc.gpsimd.dma_start(
-                wb_plane[QUADRANT * q : QUADRANT * q + PACK, :].bitcast(I32),
-                wb_scales[0, PACK * q : PACK * (q + 1), :].bitcast(I32),
-            )
         boards = []
         for t in range(PACK):
             board = keep.tile([P, C], F32, name="board%d" % t)
             nc.vector.memset(board[:], 0.0)
             boards.append(board)
-        xt_plane_all = spread_scales(xt_staged, "xt_plane_all")
-        xo_plane_all = spread_scales(xo_staged, "xo_plane_all")
-        w2_plane_plain = spread_scales(w2_staged, "w2_plane_plain")
 
-        xt_plane = keep.tile([P, J], U8, align_bytes=64)
-        nc.vector.tensor_copy(xt_plane[:], xt_plane_all[:].indirect(list1[:]))
+        xt_scales_picked = keep.tile([P, J], U8, align_bytes=64)
+        nc.vector.tensor_copy(xt_scales_picked[:], xt_scales_all[:].indirect(list1[:]))
+        xt_plane = close_up(xt_scales_picked, "xt_plane")
+        xo_scales_picked = keep.tile([P, J], U8, align_bytes=64)
+        nc.vector.tensor_copy(xo_scales_picked[:], xo_scales_all[:].indirect(list4[:]))
+        xo_plane = close_up(xo_scales_picked, "xo_plane")
         w2_plane = keep.tile([P, R], U8, align_bytes=64)
         nc.vector.tensor_copy(
             w2_plane[:].rearrange("p (t m) -> p t m", t=PACK), w2_plane_plain[:].rearrange("p (m t) -> p t m", t=PACK)
         )
-        xo_plane = keep.tile([P, J], U8, align_bytes=64)
-        nc.vector.tensor_copy(xo_plane[:], xo_plane_all[:].indirect(list4[:]))
 
         grouped = [keep.tile([P, P, PACK], BF16, name="grouped%d" % u, align_bytes=64) for u in range(PACK)]
         paired = [None] + [keep.tile([P, 2, P, 2], BF16, name="paired%d" % u) for u in range(1, PACK)]
@@ -138,7 +141,6 @@ def tile_picked_tokens_codegap_two_answered_one_plain_kernel(
             nc.scalar.activation(minus[:], tables[t][:].indirect(list3[:]), COPY, scale=step_b[:, t : t + 1])
             if t == PACK - 1:
                 nc.vector.tensor_copy(xt_codes[:], xt_all[:].indirect(list1[:]))
-                nc.vector.tensor_copy(xo_codes[:], xo_all[:].indirect(list4[:]))
             if t < PACK - 1:
                 for u in range(PACK):
                     take_off(t, u, plus, minus)
@@ -161,6 +163,7 @@ def tile_picked_tokens_codegap_two_answered_one_plain_kernel(
             nc.scalar.copy(staged[:], first[:])
             first_sb.append(staged)
 
+        nc.vector.tensor_copy(xo_codes[:], xo_all[:].indirect(list4[:]))
         w2_codes = keep.tile([P, 2 * R], U8, name="w2_codes", tag="plus%d" % (PACK - 1), align_bytes=64)
         nc.scalar.copy(
             w2_codes[:].bitcast(U16).rearrange("p (t m) -> p t m", t=PACK),

from contextlib import ExitStack

import concourse.mybir as mybir

K, J, R, T, F, Z, M, O, C, N = 512, 256, 512, 512, 2048, 512, 1024, 128, 512, 256
FLOPS = 2 * (K * R * J + Z * R * J + R * N * O)

F32 = mybir.dt.float32
BF16 = mybir.dt.bfloat16
I32 = mybir.dt.int32
U32 = mybir.dt.uint32
U16 = mybir.dt.uint16
U8 = mybir.dt.uint8
FP8X4 = mybir.dt.float8_e4m3fn_x4
FP4X4 = mybir.dt.float4_e2m1fn_x4
COPY = mybir.ActivationFunctionType.Copy
SUBTRACT = mybir.AluOpType.subtract
LARGER = mybir.AluOpType.max

P = 128
PACK = 4
QUADRANT = 32
APART = 8


def tile_picked_tokens_codegap_two_answered_one_plain_kernel(
    tc, xt_words, xt_scales, ua, ha, hb, xo_words, xo_scales, w2_words, w2_scales, sa, sb, wb_words, wb_scales,
    offs, offs2, offs3, offs4, offs5, offs6, offs7, out,
):
    nc = tc.nc
    with ExitStack() as ctx:
        keep = ctx.enter_context(tc.tile_pool(name="keep", bufs=1))
        psum = ctx.enter_context(tc.psum_pool(name="psum", bufs=1))

        def load_list(source, name):
            tile = keep.tile(list(source.shape), U16, name=name)
            nc.sync.dma_start(tile[:], source)
            return tile

        def load_rowwise(source, name, queue):
            tile = keep.tile([P, PACK], F32, name=name)
            queue.dma_start(tile[:], source.rearrange("(p t) one -> p (t one)", t=PACK))
            return tile

        def load_scales_apart(source, name, queue):
            tile = keep.tile([P, source.shape[2]], U8, name=name, align_bytes=64)
            nc.gpsimd.memset(tile[:].bitcast(I32), 0)
            queue.dma_start(tile[::APART, :].bitcast(I32), source[0].bitcast(I32))
            return tile

        def load_plane(source, name):
            plane = keep.tile([P, source.shape[2]], U8, name=name, align_bytes=64)
            nc.gpsimd.memset(plane[:].bitcast(I32), 0)
            rows = source[0].bitcast(I32).rearrange("(q i) w -> i q w", i=PACK)
            for i in range(PACK):
                nc.sync.dma_start(plane[i::QUADRANT, :].bitcast(I32), rows[i])
            return plane

        def close_up(apart, name):
            plane = keep.tile(list(apart.shape), U8, name=name, align_bytes=64)
            nc.vector.memset(plane[:].bitcast(I32), 0)
            for q in range(0, P, QUADRANT):
                nc.gpsimd.dma_start(plane[q : q + PACK, :].bitcast(I32), apart[q : q + QUADRANT : APART, :].bitcast(I32))
            return plane

        def load_table(t):
            tile = keep.tile([P, F], F32, name="table%d" % t)
            nc.sync.dma_start(tile[:], ua.rearrange("(p t) f -> t p f", t=PACK)[t])
            return tile

        def load_words(source, name):
            tile = keep.tile([P, source.shape[2]], U32, name=name, align_bytes=64)
            nc.sync.dma_start(tile[:].bitcast(I32), source[0].rearrange("p c t -> p (c t)").bitcast(I32))
            return tile

        def load_nibbles(source, name):
            tile = keep.tile([P, source.shape[2]], U8, name=name, align_bytes=64)
            nc.sync.dma_start(tile[:].bitcast(I32), source[0].bitcast(I32))
            return tile

        warm = keep.tile([P, 2], F32)
        nc.vector.memset(warm[:, 0:1], 0.0)
        nc.scalar.activation(warm[:, 1:2], warm[:, 0:1], COPY)
        tables = [load_table(0)]
        step_a = load_rowwise(ha, "step_a", nc.scalar)
        list2 = load_list(offs2, "list2")
        step_b = load_rowwise(hb, "step_b", nc.scalar)
        list3 = load_list(offs3, "list3")
        list1 = load_list(offs, "list1")
        xt_scales_all = load_scales_apart(xt_scales, "xt_scales_all", nc.scalar)
        tables.append(load_table(1))
        list4 = load_list(offs4, "list4")
        xo_scales_all = load_scales_apart(xo_scales, "xo_scales_all", nc.sync)
        w2_plane_plain = load_plane(w2_scales, "w2_plane_plain")
        tables.append(load_table(2))
        tables.append(load_table(3))
        xt_all = load_words(xt_words, "xt_all")
        xo_all = load_words(xo_words, "xo_all")
        list5 = load_list(offs5, "list5")
        w2_plain = load_nibbles(w2_words, "w2_plain")
        weight_a = load_rowwise(sa, "weight_a", nc.sync)
        list6 = load_list(offs6, "list6")
        list7 = load_list(offs7, "list7")
        weight_b = load_rowwise(sb, "weight_b", nc.sync)
        wb_codes = load_nibbles(wb_words, "wb_codes")
        wb_plane = load_plane(wb_scales, "wb_plane")

        boards = []
        for t in range(PACK):
            board = keep.tile([P, C], F32, name="board%d" % t)
            nc.vector.memset(board[:], 0.0)
            boards.append(board)

        xt_scales_picked = keep.tile([P, J], U8, align_bytes=64)
        nc.vector.tensor_copy(xt_scales_picked[:], xt_scales_all[:].indirect(list1[:]))
        xt_plane = close_up(xt_scales_picked, "xt_plane")
        xo_scales_picked = keep.tile([P, J], U8, align_bytes=64)
        nc.vector.tensor_copy(xo_scales_picked[:], xo_scales_all[:].indirect(list4[:]))
        xo_plane = close_up(xo_scales_picked, "xo_plane")
        w2_plane = keep.tile([P, R], U8, align_bytes=64)
        nc.vector.tensor_copy(
            w2_plane[:].rearrange("p (t m) -> p t m", t=PACK), w2_plane_plain[:].rearrange("p (m t) -> p t m", t=PACK)
        )

        grouped = [keep.tile([P, P, PACK], BF16, name="grouped%d" % u, align_bytes=64) for u in range(PACK)]
        paired = [None] + [keep.tile([P, 2, P, 2], BF16, name="paired%d" % u) for u in range(1, PACK)]
        wc_codes = [keep.tile([P, P], U32, name="wc_codes%d" % u, align_bytes=64) for u in range(PACK)]
        wc_plane = [keep.tile([P, P], U8, name="wc_plane%d" % u, align_bytes=64) for u in range(PACK)]
        xt_codes = keep.tile([P, J], U32, align_bytes=64)
        xo_codes = keep.tile([P, J], U32, align_bytes=64)
        first_sb = []

        def take_off(t, u, plus, minus):
            target = grouped[0][:, :, t] if u == 0 else paired[u][:, t // 2, :, t % 2]
            nc.vector.tensor_tensor(target, plus[:, u::PACK], minus[:, u::PACK], SUBTRACT)

        for t in range(PACK):
            plus = keep.tile([P, R], F32, name="plus%d" % t, tag="plus%d" % t, align_bytes=64)
            minus = keep.tile([P, R], F32, name="minus%d" % t)
            nc.scalar.activation(plus[:], tables[t][:].indirect(list2[:]), COPY, scale=step_a[:, t : t + 1])
            nc.scalar.activation(minus[:], tables[t][:].indirect(list3[:]), COPY, scale=step_b[:, t : t + 1])
            if t == PACK - 1:
                nc.vector.tensor_copy(xt_codes[:], xt_all[:].indirect(list1[:]))
            if t < PACK - 1:
                for u in range(PACK):
                    take_off(t, u, plus, minus)
        for u in range(PACK):
            take_off(PACK - 1, u, plus, minus)
            if u > 0:
                nc.scalar.copy(
                    grouped[u][:].rearrange("p m t -> p (m t)").bitcast(U32).rearrange("p (m h) -> p m h", h=2),
                    paired[u][:].rearrange("p h m e -> p (h m e)").bitcast(U32).rearrange("p (h m) -> p m h", h=2),
                )
            nc.vector.quantize_mx(
                out=wc_codes[u][:].bitcast(FP8X4), scales=wc_plane[u][:], in_=grouped[u][:].rearrange("p m t -> p (m t)")
            )
            first = psum.tile([P, J], F32, name="first%d" % u)
            nc.tensor.matmul_mx(
                out=first[:], lhsT=wc_codes[u][:].bitcast(FP8X4), lhsT_scale=wc_plane[u][:],
                rhs=xt_codes[:].bitcast(FP8X4), rhs_scale=xt_plane[:], start=True, stop=True,
            )
            staged = keep.tile([P, J], F32, name="first_sb%d" % u)
            nc.scalar.copy(staged[:], first[:])
            first_sb.append(staged)

        nc.vector.tensor_copy(xo_codes[:], xo_all[:].indirect(list4[:]))
        w2_codes = keep.tile([P, 2 * R], U8, name="w2_codes", tag="plus%d" % (PACK - 1), align_bytes=64)
        nc.scalar.copy(
            w2_codes[:].bitcast(U16).rearrange("p (t m) -> p t m", t=PACK),
            w2_plain[:].bitcast(U16).rearrange("p (m t) -> p t m", t=PACK),
        )
        second = [psum.tile([P, 2, J], F32, name="second%d" % h) for h in range(2)]
        for u in range(PACK):
            nc.tensor.matmul_mx(
                out=second[u // 2][:, u % 2, :], lhsT=w2_codes[:, 2 * P * u : 2 * P * (u + 1)].bitcast(FP4X4),
                lhsT_scale=w2_plane[:, P * u : P * (u + 1)],
                rhs=xo_codes[:].bitcast(FP8X4), rhs_scale=xo_plane[:], start=True, stop=True,
            )

        for u in range(PACK):
            nc.vector.tensor_copy(boards[u][:].indirect(list5[:]), first_sb[u][:])
        read = []
        for u in range(PACK):
            tile = keep.tile([P, J], F32, name="read%d" % u)
            nc.scalar.activation(tile[:], boards[u][:].indirect(list6[:]), COPY, scale=weight_a[:, u : u + 1])
            read.append(tile)
        hid = keep.tile([P, PACK, O], BF16)
        for u in range(PACK):
            answer = keep.tile([P, J], F32, name="answer%d" % u)
            nc.vector.tensor_tensor(answer[:], read[u][:], second[u // 2][:, u % 2, :], LARGER)
            nc.scalar.activation(hid[:, u, :], answer[:].indirect(list7[:]), COPY, scale=weight_b[:, u : u + 1])

        hid_grouped = keep.tile([P, O, PACK], BF16, align_bytes=64)
        nc.vector.tensor_copy(hid_grouped[:, :, : PACK - 1], hid[:, : PACK - 1, :].rearrange("p t o -> p o t"))
        nc.vector.tensor_copy(hid_grouped[:, :, PACK - 1], hid[:, PACK - 1, :])
        hid_codes = keep.tile([P, O], U32, align_bytes=64)
        hid_plane = keep.tile([P, O], U8, align_bytes=64)
        nc.vector.quantize_mx(
            out=hid_codes[:].bitcast(FP8X4), scales=hid_plane[:], in_=hid_grouped[:].rearrange("p o t -> p (o t)")
        )
        for h in range(N // P):
            result = psum.tile([P, O], F32, name="result%d" % h)
            nc.tensor.matmul_mx(
                out=result[:], lhsT=wb_codes[:, 2 * P * h : 2 * P * (h + 1)].bitcast(FP4X4),
                lhsT_scale=wb_plane[:, P * h : P * (h + 1)],
                rhs=hid_codes[:].bitcast(FP8X4), rhs_scale=hid_plane[:], start=True, stop=True,
            )
            result_sb = keep.tile([P, O], F32, name="result_sb%d" % h)
            if h == 0:
                nc.scalar.copy(result_sb[:], result[:])
                nc.scalar.dma_start(out[P * h : P * (h + 1), :], result_sb[:])
            else:
                nc.vector.tensor_copy(result_sb[:], result[:])
                nc.sync.dma_start(out[P * h : P * (h + 1), :], result_sb[:])
